import numpy as np
import ml_dtypes


def mxq(x, axis, fmt="e4m3"):
    dtype, down = {"e4m3": (ml_dtypes.float8_e4m3fn, 7), "e5m2": (ml_dtypes.float8_e5m2, 14)}[fmt]
    v = np.moveaxis(np.asarray(x, np.float32).astype(ml_dtypes.bfloat16).astype(np.float64), axis, -1)
    blocks = v.reshape(v.shape[:-1] + (-1, 32))
    amax = np.abs(blocks).max(-1, keepdims=True)
    byte = np.maximum(np.where(amax > 0, np.frexp(amax)[1] - 1 + 127, 0) - down, 1)
    scale = np.exp2(byte - 127.0)
    codes = (blocks / scale).astype(np.float32).astype(dtype).astype(np.float64)
    return np.moveaxis((codes * scale).reshape(v.shape), -1, axis)


WIDE = False


def mx_kscale(k):
    if not WIDE:
        return np.ones(k)
    levels = np.array([10, -10, 5, -5, 0])
    if k % 512:
        return np.exp2(np.random.permutation(np.resize(levels, k // 32))).repeat(32)
    a = np.empty((k // 512, 16))
    for p in range(k // 512):
        a[p, :8] = np.random.permutation(np.resize(levels, 8))
        for g in range(8):
            far = levels[np.abs(levels - a[p, g]) >= 10]
            a[p, g + 8] = far[np.random.randint(len(far))]
    return np.exp2(a.ravel()).repeat(32)


def f64(x):
    return np.asarray(x).astype(np.float64)


def striped(idx):
    return np.tile(idx.reshape(-1, 16).T, (8, 1)).astype(np.uint16)


def unstriped(offs):
    return offs[:16].T.reshape(-1).astype(np.int64)


E2M1 = np.array([0.0, 0.5, 1.0, 1.5, 2.0, 3.0, 4.0, 6.0, -0.0, -0.5, -1.0, -1.5, -2.0, -3.0, -4.0, -6.0])


def pack_weight(w, fmt):
    k, n = w.shape
    w = f64(np.asarray(w, np.float32).astype(ml_dtypes.bfloat16)).reshape(k // 32, 32, n)
    amax = np.abs(w).max(1)
    if fmt == "e4m3":
        byte = np.frexp(amax)[1] - 1 + 127 - 7
    else:
        mant, ex = np.frexp(amax / 6.0)
        byte = np.where(mant > 0.5, ex, ex - 1) + 127
    byte = np.clip(np.where(amax > 0, byte, 1), 1, 254)
    scaled = (w * np.exp2(127.0 - byte)[:, None, :]).reshape(k, n).astype(np.float32)
    by_word = np.ascontiguousarray(scaled.reshape(k // 512, 128, 4, n).transpose(0, 1, 3, 2))
    if fmt == "e4m3":
        words = by_word.astype(ml_dtypes.float8_e4m3fn).view(np.uint8)
    else:
        c = by_word.astype(ml_dtypes.float4_e2m1fn).view(np.uint8) & 0xF
        words = (c[..., 0::2] | (c[..., 1::2] << 4)).reshape(k // 512, 128, 2 * n)
    return np.ascontiguousarray(words), np.ascontiguousarray(byte.astype(np.uint8).reshape(k // 512, 16, n))


def unpack_weight(words, scales, fmt):
    g, _, n = scales.shape
    words = np.ascontiguousarray(words).reshape(g, 128, n, -1)
    if fmt == "e4m3":
        vals = words.view(ml_dtypes.float8_e4m3fn).astype(np.float64)
    else:
        nib = np.empty((g, 128, n, 4), np.uint8)
        nib[..., 0::2] = words & 0xF
        nib[..., 1::2] = words >> 4
        vals = E2M1[nib]
    vals = vals * np.repeat(np.exp2(scales.astype(np.float64) - 127.0), 8, axis=1)[..., None]
    return vals.transpose(0, 1, 3, 2).reshape(g * 512, n)


def gelu(v):
    return 0.5 * v * (1.0 + np.tanh(np.sqrt(2.0 / np.pi) * (v + 0.044715 * v**3)))


K, H, T, S, T2, T3, S2, P = 512, 1024, 2048, 1024, 2048, 2048, 1024, 512

def setup_inputs():
    n = np.random.standard_normal
    s = mx_kscale(K)[:, None]
    u = mx_kscale(H)[:, None]
    tab_words, tab_scales = pack_weight(n((K, T)) * s, "e4m3")
    tab2_words, tab2_scales = pack_weight(2.0 * n((H, T3)) / np.sqrt(H) / u, "e4m3")
    w2_words, w2_scales = pack_weight(1.4 * n((K, H)) / np.sqrt(K) / s * u.T, "e2m1")
    return {
        "tab_words": tab_words, "tab_scales": tab_scales,
        "tab2_words": tab2_words, "tab2_scales": tab2_scales,
        "w1": (1.4 * n((K, H)) / np.sqrt(K) / s * u.T).astype(np.float32),
        "w2_words": w2_words, "w2_scales": w2_scales,
        "w3": (1.5 * n((K, H)) / np.sqrt(K) / s).astype(np.float32),
        "wgs": np.exp(0.3 * n((128, S))).astype(np.float32),
        "page0": (n((H, T2)) * u).astype(np.float32),
        "consent": np.random.uniform(0.2, 1.5, (S2, P)).astype(np.float32),
        "offs": striped(np.random.permutation(T)[:S]),
        "offs2": striped(np.random.permutation(T3)[:S2]),
        "offs3": striped(np.random.permutation(T2)[:S]),
        "offs4": striped(np.random.permutation(T2)[:P]),
    }

def reference(tab_words, tab_scales, tab2_words, tab2_scales, w1, w2_words, w2_scales, w3,
              wgs, page0, consent, offs, offs2, offs3, offs4):
    v = unpack_weight(tab_words, tab_scales, "e4m3")[:, unstriped(offs)]
    w2 = unpack_weight(w2_words, w2_scales, "e2m1")
    y1 = mxq(f64(w1), 0, "e4m3").T @ v
    y2 = w2.T @ v
    y3 = mxq(f64(w3), 0, "e4m3").T @ v
    h = np.maximum(y1, y2) * np.tanh(y3)
    page = f64(page0).copy()
    page[:, unstriped(offs3)] = np.tile(f64(wgs), (H // 128, 1)) * h
    x = np.abs(page[:, unstriped(offs4)])
    v2 = unpack_weight(tab2_words, tab2_scales, "e4m3")[:, unstriped(offs2)]
    e = v2.T @ mxq(x, 0, "e4m3")
    score = 1.0 / (1.0 + np.exp(-e))
    return score * f64(consent)

@@ -1,0 +1,245 @@
+from contextlib import ExitStack
+
+import concourse.mybir as mybir
+
+K, H, T, S, T2, S2, NP = 512, 1024, 2048, 1024, 2048, 1024, 512
+FLOPS = 3 * 2 * K * H * S + 2 * H * S2 * NP
+
+F32 = mybir.dt.float32
+BF16 = mybir.dt.bfloat16
+I32 = mybir.dt.int32
+U32 = mybir.dt.uint32
+U16 = mybir.dt.uint16
+U8 = mybir.dt.uint8
+FP8X4 = mybir.dt.float8_e4m3fn_x4
+FP4X4 = mybir.dt.float4_e2m1fn_x4
+ALU = mybir.AluOpType
+ACT = mybir.ActivationFunctionType
+
+P = 128
+PACK = 4
+RUN = P * PACK
+BANK = 512
+HALF = NP // 2
+SLICES = H // P
+
+
+def tile_list_archive_passage_finder_kernel(
+    tc, tab_words, tab_scales, tab2_words, tab2_scales, w1, w2_words, w2_scales, w3,
+    wgs, page0, consent, offs, offs2, offs3, offs4, out,
+):
+    nc = tc.nc
+    with ExitStack() as ctx:
+        keep = ctx.enter_context(tc.tile_pool(name="keep", bufs=1))
+        raws = ctx.enter_context(tc.tile_pool(name="raws", bufs=4))
+        pages = ctx.enter_context(tc.tile_pool(name="pages", bufs=4))
+        work = ctx.enter_context(tc.tile_pool(name="work", bufs=2))
+        feats = ctx.enter_context(tc.tile_pool(name="feats", bufs=3))
+        psum = ctx.enter_context(tc.psum_pool(name="psum", bufs=1))
+
+        def kept(shape, dtype, name):
+            return keep.tile(shape, dtype, name=name, align_bytes=64)
+
+        def load_list(src, name):
+            tile = keep.tile(list(src.shape), U16, name=name)
+            nc.sync.dma_start(tile[:], src)
+            return tile
+
+        def zeroed_plane(width, name):
+            tile = kept([P, width], U8, name)
+            nc.vector.memset(tile[:].bitcast(I32), 0)
+            return tile
+
+        def load_words(src, name):
+            tile = kept([P, T], I32, name)
+            nc.sync.dma_start(tile[:], src.rearrange("p t i -> p (t i)").bitcast(I32))
+            return tile
+
+        def load_weight(w, a):
+            tile = raws.tile([P, PACK, RUN], F32, name="raw")
+            nc.sync.dma_start(tile[:], w.rearrange("(p j) c -> p j c", j=PACK)[:, :, a * RUN : (a + 1) * RUN])
+            return tile
+
+        def load_page(s):
+            a, t = divmod(s, PACK)
+            tile = pages.tile([P, T2], F32, name="page")
+            nc.sync.dma_start(tile[:], page0.rearrange("(a p t) c -> a t p c", p=P, t=PACK)[a, t])
+            return tile
+
+        wgs_rows = wgs.rearrange("(q t) j -> q t j", t=PACK)
+
+        def load_wgs(t0, t1, name):
+            tile = kept([P, t1 - t0, S], F32, name)
+            for q in range(4):
+                nc.sync.dma_start(tile[32 * q : 32 * q + 32], wgs_rows[:, t0:t1, :])
+            return tile
+
+        v_plane = zeroed_plane(T, "v_plane")
+        w2_plane = zeroed_plane(H, "w2_plane")
+        v2_plane = zeroed_plane(T, "v2_plane")
+        idx = load_list(offs, "idx")
+        for q in range(4):
+            nc.sync.dma_start(v_plane[32 * q : 32 * q + 4, :].bitcast(I32), tab_scales[0, 4 * q : 4 * q + 4, :].bitcast(I32))
+        w2_raw = kept([P, 2 * H], U8, "w2_raw")
+        nc.sync.dma_start(w2_raw[:].bitcast(I32), w2_words[0].bitcast(I32))
+        v_table = load_words(tab_words[0], "v_table")
+        raw = {(3, 0): load_weight(w3, 0)}
+        for q in range(4):
+            nc.sync.dma_start(w2_plane[32 * q : 32 * q + 4, :].bitcast(I32), w2_scales[0, 4 * q : 4 * q + 4, :].bitcast(I32))
+        raw[1, 0] = load_weight(w1, 0)
+        idx2 = load_list(offs2, "idx2")
+        for q in range(4):
+            nc.sync.dma_start(v2_plane[32 * q : 32 * q + 8, :].bitcast(I32), tab2_scales[:, 4 * q : 4 * q + 4, :].bitcast(I32))
+        wgs_first = load_wgs(0, 1, "wgs_first")
+        v2_table = [load_words(tab2_words[0], "v2_table0")]
+        idx3 = load_list(offs3, "idx3")
+        page = {0: load_page(0)}
+        wgs_rest = load_wgs(1, PACK, "wgs_rest")
+        idx4 = load_list(offs4, "idx4")
+        v2_table.append(load_words(tab2_words[1], "v2_table1"))
+        page[1] = load_page(1)
+        page[2] = load_page(2)
+        raw[3, 1] = load_weight(w3, 1)
+        raw[1, 1] = load_weight(w1, 1)
+        page[3] = load_page(3)
+
+        v_scales = kept([P, S], U8, "v_scales")
+        nc.vector.tensor_copy(v_scales[:], v_plane[:].indirect(idx[:]))
+        w2_codes = kept([P, 2 * H], U8, "w2_codes")
+        nc.vector.tensor_copy(
+            w2_codes[:].bitcast(U16).rearrange("p (a t m) -> p a t m", a=2, t=PACK),
+            w2_raw[:].bitcast(U16).rearrange("p (a m t) -> p a t m", a=2, t=PACK),
+        )
+        v_codes = kept([P, S], U32, "v_codes")
+        nc.vector.tensor_copy(v_codes[:], v_table[:].bitcast(U32).indirect(idx[:]))
+        w2_sc = kept([P, H], U8, "w2_sc")
+        nc.vector.tensor_copy(
+            w2_sc[:].rearrange("p (a t m) -> p a t m", a=2, t=PACK),
+            w2_plane[:].rearrange("p (a m t) -> p a t m", a=2, t=PACK),
+        )
+
+        w_codes = {n: kept([P, H], U32, "w%d_codes" % n) for n in (1, 3)}
+        w_scales = {n: kept([P, H], U8, "w%d_scales" % n) for n in (1, 3)}
+
+        def quantise_weight(n, a, t0, t1):
+            count = t1 - t0
+            grouped = work.tile([P, count * RUN], BF16, name="w_grouped", align_bytes=64)
+            nc.scalar.copy(
+                grouped[:].rearrange("p (t m j) -> p m j t", t=count, j=PACK),
+                raw[n, a][:].rearrange("p j (m t) -> p m j t", t=PACK)[:, :, :, t0:t1],
+            )
+            cols = slice(a * RUN + t0 * P, a * RUN + t1 * P)
+            nc.vector.quantize_mx(out=w_codes[n][:, cols].bitcast(FP8X4), scales=w_scales[n][:, cols], in_=grouped[:])
+
+        def bank(b):
+            return psum.tile([P, BANK], F32, name="bank%d" % b)
+
+        best = {}
+
+        def readings(s):
+            cols = slice(s * P, (s + 1) * P)
+            y2_sb = work.tile([P, S], F32, name="y2_sb")
+            tone = work.tile([P, S], F32, name="tone")
+            top = feats.tile([P, S], F32, name="top")
+            for h in range(S // BANK):
+                js = slice(h * BANK, (h + 1) * BANK)
+                moving = dict(rhs=v_codes[:, js].bitcast(FP8X4), rhs_scale=v_scales[:, js], start=True, stop=True)
+                y2 = bank(2 + h)
+                nc.tensor.matmul_mx(out=y2[:], lhsT=w2_codes[:, 2 * s * P : 2 * (s + 1) * P].bitcast(FP4X4), lhsT_scale=w2_sc[:, cols], **moving)
+                y1 = bank(6 * (s % 2) + h)
+                nc.tensor.matmul_mx(out=y1[:], lhsT=w_codes[1][:, cols].bitcast(FP8X4), lhsT_scale=w_scales[1][:, cols], **moving)
+                y3 = bank(4 + h)
+                nc.tensor.matmul_mx(out=y3[:], lhsT=w_codes[3][:, cols].bitcast(FP8X4), lhsT_scale=w_scales[3][:, cols], **moving)
+                nc.scalar.copy(y2_sb[:, js], y2[:])
+                nc.scalar.activation(tone[:, js], y3[:], ACT.Tanh)
+                nc.vector.tensor_tensor(top[:, js], y1[:], y2_sb[:, js], ALU.max)
+            t = s % PACK
+            factor = wgs_first[:, 0, :] if t == 0 else wgs_rest[:, t - 1, :]
+            nc.gpsimd.tensor_tensor(top[:], top[:], tone[:], ALU.mult)
+            nc.gpsimd.tensor_tensor(top[:], top[:], factor, ALU.mult)
+            best[s] = top
+
+        def put(s):
+            nc.vector.tensor_copy(page[s][:].indirect(idx3[:]), best[s][:])
+
+        opened = {(a, h): kept([P, PACK, HALF], F32, "opened%d%d" % (a, h)) for a in range(2) for h in range(2)}
+        x_codes = {(a, h): kept([P, HALF], U32, "x_codes%d%d" % (a, h)) for a in range(2) for h in range(2)}
+        x_scales = {(a, h): kept([P, HALF], U8, "x_scales%d%d" % (a, h)) for a in range(2) for h in range(2)}
+
+        def fetch(s):
+            a, t = divmod(s, PACK)
+            for h in range(2):
+                listed = idx4[:, h * (HALF // 16) : (h + 1) * (HALF // 16)]
+                nc.vector.tensor_copy(opened[a, h][:, t, :], page[s][:].indirect(listed))
+
+        def quantise_x(a, h):
+            grouped = work.tile([P, HALF * PACK], BF16, name="x_grouped", align_bytes=64)
+            nc.scalar.activation(
+                grouped[:].rearrange("p (c i t) -> p c t i", i=4, t=PACK),
+                opened[a, h][:].rearrange("p t (c i) -> p c t i", i=4),
+                ACT.Abs,
+            )
+            nc.vector.quantize_mx(out=x_codes[a, h][:].bitcast(FP8X4), scales=x_scales[a, h][:], in_=grouped[:])
+
+        v2_scales = kept([P, S2], U8, "v2_scales")
+        v2_codes = [kept([P, S2], U32, "v2_codes%d" % a) for a in range(2)]
+        for n in (3, 1):
+            quantise_weight(n, 0, 0, 1)
+        readings(0)
+        nc.vector.tensor_copy(v2_scales[:], v2_plane[:].indirect(idx2[:]))
+        for n in (3, 1):
+            quantise_weight(n, 0, 1, PACK)
+        readings(1)
+        nc.vector.tensor_copy(v2_codes[0][:], v2_table[0][:].bitcast(U32).indirect(idx2[:]))
+        allowed = {}
+
+        for s in range(SLICES):
+            put(s)
+            fetch(s)
+            if s + PACK < SLICES:
+                page[s + PACK] = load_page(s + PACK)
+            if s == 0:
+                nc.vector.tensor_copy(v2_codes[1][:], v2_table[1][:].bitcast(U32).indirect(idx2[:]))
+            if s == 1:
+                for n in (3, 1):
+                    quantise_weight(n, 1, 0, PACK)
+                for g in range(2):
+                    allowed[g] = raws.tile([P, PACK, NP], F32, name="raw")
+                    nc.sync.dma_start(allowed[g][:], consent.rearrange("(c p) j -> p c j", p=P)[:, PACK * g : PACK * (g + 1), :])
+                    nc.scalar.mul(allowed[g][:], allowed[g][:], 0.5)
+            if s == PACK - 1:
+                for h in range(2):
+                    quantise_x(0, h)
+            if s + 2 < SLICES:
+                readings(s + 2)
+
+        def score_pass(e, h, pair, a):
+            for i in range(2):
+                ms = slice((2 * pair + i) * P, (2 * pair + i + 1) * P)
+                nc.tensor.matmul_mx(
+                    out=e[:, i * HALF : (i + 1) * HALF],
+                    lhsT=v2_codes[a][:, ms].bitcast(FP8X4),
+                    lhsT_scale=v2_scales[4 * a : P, ms],
+                    rhs=x_codes[a, h][:].bitcast(FP8X4),
+                    rhs_scale=x_scales[a, h][:],
+                    start=(a == 0 and i == 0),
+                    stop=(a == 1 and i == 1),
+                )
+
+        sums = {}
+        for h in range(2):
+            for pair in range(4):
+                sums[h, pair] = bank(4 * h + pair)
+                score_pass(sums[h, pair], h, pair, 0)
+        for h in range(2):
+            quantise_x(1, h)
+        out_rows = out.rearrange("(c p) j -> p c j", p=P)
+        for h in range(2):
+            js = slice(h * HALF, (h + 1) * HALF)
+            for pair in range(4):
+                score_pass(sums[h, pair], h, pair, 1)
+                score = kept([P, 2, HALF], F32, "score%d%d" % (h, pair))
+                nc.scalar.activation(score[:].rearrange("p i j -> p (i j)"), sums[h, pair][:], ACT.Tanh, scale=0.5)
+                g, c = divmod(2 * pair, PACK)
+                nc.vector.scalar_tensor_tensor(score[:], score[:], 1.0, allowed[g][:, c : c + 2, js], ALU.add, ALU.mult)
+                nc.sync.dma_start(out_rows[:, 2 * pair : 2 * pair + 2, js], score[:])

@@ -32,7 +32,7 @@ def tile_list_archive_passage_finder_kernel(
     with ExitStack() as ctx:
         keep = ctx.enter_context(tc.tile_pool(name="keep", bufs=1))
         raws = ctx.enter_context(tc.tile_pool(name="raws", bufs=4))
-        pages = ctx.enter_context(tc.tile_pool(name="pages", bufs=4))
+        pages = ctx.enter_context(tc.tile_pool(name="pages", bufs=SLICES))
         work = ctx.enter_context(tc.tile_pool(name="work", bufs=2))
         feats = ctx.enter_context(tc.tile_pool(name="feats", bufs=3))
         psum = ctx.enter_context(tc.psum_pool(name="psum", bufs=1))
@@ -45,9 +45,9 @@ def tile_list_archive_passage_finder_kernel(
             nc.sync.dma_start(tile[:], src)
             return tile
 
-        def zeroed_plane(width, name):
+        def zeroed_plane(engine, width, name):
             tile = kept([P, width], U8, name)
-            nc.vector.memset(tile[:].bitcast(I32), 0)
+            engine.memset(tile[:].bitcast(I32), 0)
             return tile
 
         def load_words(src, name):
@@ -74,9 +74,9 @@ def tile_list_archive_passage_finder_kernel(
                 nc.sync.dma_start(tile[32 * q : 32 * q + 32], wgs_rows[:, t0:t1, :])
             return tile
 
-        v_plane = zeroed_plane(T, "v_plane")
-        w2_plane = zeroed_plane(H, "w2_plane")
-        v2_plane = zeroed_plane(T, "v2_plane")
+        v_plane = zeroed_plane(nc.vector, T, "v_plane")
+        w2_plane = zeroed_plane(nc.gpsimd, H, "w2_plane")
+        v2_plane = zeroed_plane(nc.gpsimd, T, "v2_plane")
         idx = load_list(offs, "idx")
         for q in range(4):
             nc.sync.dma_start(v_plane[32 * q : 32 * q + 4, :].bitcast(I32), tab_scales[0, 4 * q : 4 * q + 4, :].bitcast(I32))
@@ -94,14 +94,23 @@ def tile_list_archive_passage_finder_kernel(
         v2_table = [load_words(tab2_words[0], "v2_table0")]
         idx3 = load_list(offs3, "idx3")
         page = {0: load_page(0)}
-        wgs_rest = load_wgs(1, PACK, "wgs_rest")
+        wgs_second = load_wgs(1, 2, "wgs_second")
         idx4 = load_list(offs4, "idx4")
-        v2_table.append(load_words(tab2_words[1], "v2_table1"))
         page[1] = load_page(1)
-        page[2] = load_page(2)
         raw[3, 1] = load_weight(w3, 1)
         raw[1, 1] = load_weight(w1, 1)
-        page[3] = load_page(3)
+        wgs_rest = load_wgs(2, PACK, "wgs_rest")
+        factors = [wgs_first[:, 0, :], wgs_second[:, 0, :], wgs_rest[:, 0, :], wgs_rest[:, 1, :]]
+        v2_table.append(load_words(tab2_words[1], "v2_table1"))
+        for s in range(2, PACK):
+            page[s] = load_page(s)
+        allowed = []
+        for g in range(2):
+            tile = raws.tile([P, PACK, NP], F32, name="raw")
+            nc.sync.dma_start(tile[:], consent.rearrange("(c p) j -> p c j", p=P)[:, PACK * g : PACK * (g + 1), :])
+            allowed.append(tile)
+        for s in range(PACK, SLICES):
+            page[s] = load_page(s)
 
         v_scales = kept([P, S], U8, "v_scales")
         nc.vector.tensor_copy(v_scales[:], v_plane[:].indirect(idx[:]))
@@ -121,10 +130,10 @@ def tile_list_archive_passage_finder_kernel(
         w_codes = {n: kept([P, H], U32, "w%d_codes" % n) for n in (1, 3)}
         w_scales = {n: kept([P, H], U8, "w%d_scales" % n) for n in (1, 3)}
 
-        def quantise_weight(n, a, t0, t1):
+        def quantise_weight(copy, n, a, t0, t1):
             count = t1 - t0
-            grouped = work.tile([P, count * RUN], BF16, name="w_grouped", align_bytes=64)
-            nc.scalar.copy(
+            grouped = work.tile([P, count * RUN], BF16, name="first_grouped" if count == 1 else "grouped", align_bytes=64)
+            copy(
                 grouped[:].rearrange("p (t m j) -> p m j t", t=count, j=PACK),
                 raw[n, a][:].rearrange("p j (m t) -> p m j t", t=PACK)[:, :, :, t0:t1],
             )
@@ -139,7 +148,7 @@ def tile_list_archive_passage_finder_kernel(
         def readings(s):
             cols = slice(s * P, (s + 1) * P)
             y2_sb = work.tile([P, S], F32, name="y2_sb")
-            tone = work.tile([P, S], F32, name="tone")
+            tone = keep.tile([P, S], F32, name="tone")
             top = feats.tile([P, S], F32, name="top")
             for h in range(S // BANK):
                 js = slice(h * BANK, (h + 1) * BANK)
@@ -153,10 +162,8 @@ def tile_list_archive_passage_finder_kernel(
                 nc.scalar.copy(y2_sb[:, js], y2[:])
                 nc.scalar.activation(tone[:, js], y3[:], ACT.Tanh)
                 nc.vector.tensor_tensor(top[:, js], y1[:], y2_sb[:, js], ALU.max)
-            t = s % PACK
-            factor = wgs_first[:, 0, :] if t == 0 else wgs_rest[:, t - 1, :]
+            nc.gpsimd.tensor_tensor(tone[:], tone[:], factors[s % PACK], ALU.mult)
             nc.gpsimd.tensor_tensor(top[:], top[:], tone[:], ALU.mult)
-            nc.gpsimd.tensor_tensor(top[:], top[:], factor, ALU.mult)
             best[s] = top
 
         def put(s):
@@ -173,7 +180,7 @@ def tile_list_archive_passage_finder_kernel(
                 nc.vector.tensor_copy(opened[a, h][:, t, :], page[s][:].indirect(listed))
 
         def quantise_x(a, h):
-            grouped = work.tile([P, HALF * PACK], BF16, name="x_grouped", align_bytes=64)
+            grouped = work.tile([P, HALF * PACK], BF16, name="grouped", align_bytes=64)
             nc.scalar.activation(
                 grouped[:].rearrange("p (c i t) -> p c t i", i=4, t=PACK),
                 opened[a, h][:].rearrange("p t (c i) -> p c t i", i=4),
@@ -184,28 +191,23 @@ def tile_list_archive_passage_finder_kernel(
         v2_scales = kept([P, S2], U8, "v2_scales")
         v2_codes = [kept([P, S2], U32, "v2_codes%d" % a) for a in range(2)]
         for n in (3, 1):
-            quantise_weight(n, 0, 0, 1)
+            quantise_weight(nc.vector.tensor_copy, n, 0, 0, 1)
         readings(0)
         nc.vector.tensor_copy(v2_scales[:], v2_plane[:].indirect(idx2[:]))
         for n in (3, 1):
-            quantise_weight(n, 0, 1, PACK)
+            quantise_weight(nc.scalar.copy, n, 0, 1, PACK)
         readings(1)
         nc.vector.tensor_copy(v2_codes[0][:], v2_table[0][:].bitcast(U32).indirect(idx2[:]))
-        allowed = {}
 
         for s in range(SLICES):
             put(s)
             fetch(s)
-            if s + PACK < SLICES:
-                page[s + PACK] = load_page(s + PACK)
             if s == 0:
                 nc.vector.tensor_copy(v2_codes[1][:], v2_table[1][:].bitcast(U32).indirect(idx2[:]))
-            if s == 1:
                 for n in (3, 1):
-                    quantise_weight(n, 1, 0, PACK)
+                    quantise_weight(nc.scalar.copy, n, 1, 0, PACK)
+            if s == PACK:
                 for g in range(2):
-                    allowed[g] = raws.tile([P, PACK, NP], F32, name="raw")
-                    nc.sync.dma_start(allowed[g][:], consent.rearrange("(c p) j -> p c j", p=P)[:, PACK * g : PACK * (g + 1), :])
                     nc.scalar.mul(allowed[g][:], allowed[g][:], 0.5)
             if s == PACK - 1:
                 for h in range(2):
@@ -238,8 +240,11 @@ def tile_list_archive_passage_finder_kernel(
             js = slice(h * HALF, (h + 1) * HALF)
             for pair in range(4):
                 score_pass(sums[h, pair], h, pair, 1)
-                score = kept([P, 2, HALF], F32, "score%d%d" % (h, pair))
-                nc.scalar.activation(score[:].rearrange("p i j -> p (i j)"), sums[h, pair][:], ACT.Tanh, scale=0.5)
+                score = pages.tile([P, 2, HALF], F32, name="page")
                 g, c = divmod(2 * pair, PACK)
-                nc.vector.scalar_tensor_tensor(score[:], score[:], 1.0, allowed[g][:, c : c + 2, js], ALU.add, ALU.mult)
-                nc.sync.dma_start(out_rows[:, 2 * pair : 2 * pair + 2, js], score[:])
+                last = h == 1 and pair == 3
+                for i0, i1 in ((0, 1), (1, 2)) if last else ((0, 2),):
+                    part = score[:, i0:i1, :]
+                    nc.scalar.activation(part.rearrange("p i j -> p (i j)"), sums[h, pair][:, i0 * HALF : i1 * HALF], ACT.Tanh, scale=0.5)
+                    nc.vector.scalar_tensor_tensor(part, part, 1.0, allowed[g][:, c + i0 : c + i1, js], ALU.add, ALU.mult)
+                    nc.sync.dma_start(out_rows[:, 2 * pair + i0 : 2 * pair + i1, js], part)

from contextlib import ExitStack

import concourse.mybir as mybir

K, H, T, S, T2, S2, NP = 512, 1024, 2048, 1024, 2048, 1024, 512
FLOPS = 3 * 2 * K * H * S + 2 * H * S2 * NP

F32 = mybir.dt.float32
BF16 = mybir.dt.bfloat16
I32 = mybir.dt.int32
U32 = mybir.dt.uint32
U16 = mybir.dt.uint16
U8 = mybir.dt.uint8
FP8X4 = mybir.dt.float8_e4m3fn_x4
FP4X4 = mybir.dt.float4_e2m1fn_x4
ALU = mybir.AluOpType
ACT = mybir.ActivationFunctionType

P = 128
PACK = 4
RUN = P * PACK
BANK = 512
HALF = NP // 2
SLICES = H // P


def tile_list_archive_passage_finder_kernel(
    tc, tab_words, tab_scales, tab2_words, tab2_scales, w1, w2_words, w2_scales, w3,
    wgs, page0, consent, offs, offs2, offs3, offs4, out,
):
    nc = tc.nc
    with ExitStack() as ctx:
        keep = ctx.enter_context(tc.tile_pool(name="keep", bufs=1))
        raws = ctx.enter_context(tc.tile_pool(name="raws", bufs=4))
        pages = ctx.enter_context(tc.tile_pool(name="pages", bufs=SLICES))
        work = ctx.enter_context(tc.tile_pool(name="work", bufs=2))
        feats = ctx.enter_context(tc.tile_pool(name="feats", bufs=3))
        psum = ctx.enter_context(tc.psum_pool(name="psum", bufs=1))

        def kept(shape, dtype, name):
            return keep.tile(shape, dtype, name=name, align_bytes=64)

        def load_list(src, name):
            tile = keep.tile(list(src.shape), U16, name=name)
            nc.sync.dma_start(tile[:], src)
            return tile

        def zeroed_plane(engine, width, name):
            tile = kept([P, width], U8, name)
            engine.memset(tile[:].bitcast(I32), 0)
            return tile

        def load_words(src, name):
            tile = kept([P, T], I32, name)
            nc.sync.dma_start(tile[:], src.rearrange("p t i -> p (t i)").bitcast(I32))
            return tile

        def load_weight(w, a):
            tile = raws.tile([P, PACK, RUN], F32, name="raw")
            nc.sync.dma_start(tile[:], w.rearrange("(p j) c -> p j c", j=PACK)[:, :, a * RUN : (a + 1) * RUN])
            return tile

        def load_page(s):
            a, t = divmod(s, PACK)
            tile = pages.tile([P, T2], F32, name="page")
            nc.sync.dma_start(tile[:], page0.rearrange("(a p t) c -> a t p c", p=P, t=PACK)[a, t])
            return tile

        wgs_rows = wgs.rearrange("(q t) j -> q t j", t=PACK)

        def load_wgs(t0, t1, name):
            tile = kept([P, t1 - t0, S], F32, name)
            for q in range(4):
                nc.sync.dma_start(tile[32 * q : 32 * q + 32], wgs_rows[:, t0:t1, :])
            return tile

        v_plane = zeroed_plane(nc.vector, T, "v_plane")
        w2_plane = zeroed_plane(nc.gpsimd, H, "w2_plane")
        v2_plane = zeroed_plane(nc.gpsimd, T, "v2_plane")
        idx = load_list(offs, "idx")
        for q in range(4):
            nc.sync.dma_start(v_plane[32 * q : 32 * q + 4, :].bitcast(I32), tab_scales[0, 4 * q : 4 * q + 4, :].bitcast(I32))
        w2_raw = kept([P, 2 * H], U8, "w2_raw")
        nc.sync.dma_start(w2_raw[:].bitcast(I32), w2_words[0].bitcast(I32))
        v_table = load_words(tab_words[0], "v_table")
        raw = {(3, 0): load_weight(w3, 0)}
        for q in range(4):
            nc.sync.dma_start(w2_plane[32 * q : 32 * q + 4, :].bitcast(I32), w2_scales[0, 4 * q : 4 * q + 4, :].bitcast(I32))
        raw[1, 0] = load_weight(w1, 0)
        idx2 = load_list(offs2, "idx2")
        for q in range(4):
            nc.sync.dma_start(v2_plane[32 * q : 32 * q + 8, :].bitcast(I32), tab2_scales[:, 4 * q : 4 * q + 4, :].bitcast(I32))
        wgs_first = load_wgs(0, 1, "wgs_first")
        v2_table = [load_words(tab2_words[0], "v2_table0")]
        idx3 = load_list(offs3, "idx3")
        page = {0: load_page(0)}
        wgs_second = load_wgs(1, 2, "wgs_second")
        idx4 = load_list(offs4, "idx4")
        page[1] = load_page(1)
        raw[3, 1] = load_weight(w3, 1)
        raw[1, 1] = load_weight(w1, 1)
        wgs_rest = load_wgs(2, PACK, "wgs_rest")
        factors = [wgs_first[:, 0, :], wgs_second[:, 0, :], wgs_rest[:, 0, :], wgs_rest[:, 1, :]]
        v2_table.append(load_words(tab2_words[1], "v2_table1"))
        for s in range(2, PACK):
            page[s] = load_page(s)
        allowed = []
        for g in range(2):
            tile = raws.tile([P, PACK, NP], F32, name="raw")
            nc.sync.dma_start(tile[:], consent.rearrange("(c p) j -> p c j", p=P)[:, PACK * g : PACK * (g + 1), :])
            allowed.append(tile)
        for s in range(PACK, SLICES):
            page[s] = load_page(s)

        v_scales = kept([P, S], U8, "v_scales")
        nc.vector.tensor_copy(v_scales[:], v_plane[:].indirect(idx[:]))
        w2_codes = kept([P, 2 * H], U8, "w2_codes")
        nc.vector.tensor_copy(
            w2_codes[:].bitcast(U16).rearrange("p (a t m) -> p a t m", a=2, t=PACK),
            w2_raw[:].bitcast(U16).rearrange("p (a m t) -> p a t m", a=2, t=PACK),
        )
        v_codes = kept([P, S], U32, "v_codes")
        nc.vector.tensor_copy(v_codes[:], v_table[:].bitcast(U32).indirect(idx[:]))
        w2_sc = kept([P, H], U8, "w2_sc")
        nc.vector.tensor_copy(
            w2_sc[:].rearrange("p (a t m) -> p a t m", a=2, t=PACK),
            w2_plane[:].rearrange("p (a m t) -> p a t m", a=2, t=PACK),
        )

        w_codes = {n: kept([P, H], U32, "w%d_codes" % n) for n in (1, 3)}
        w_scales = {n: kept([P, H], U8, "w%d_scales" % n) for n in (1, 3)}

        def quantise_weight(copy, n, a, t0, t1):
            count = t1 - t0
            grouped = work.tile([P, count * RUN], BF16, name="first_grouped" if count == 1 else "grouped", align_bytes=64)
            copy(
                grouped[:].rearrange("p (t m j) -> p m j t", t=count, j=PACK),
                raw[n, a][:].rearrange("p j (m t) -> p m j t", t=PACK)[:, :, :, t0:t1],
            )
            cols = slice(a * RUN + t0 * P, a * RUN + t1 * P)
            nc.vector.quantize_mx(out=w_codes[n][:, cols].bitcast(FP8X4), scales=w_scales[n][:, cols], in_=grouped[:])

        def bank(b):
            return psum.tile([P, BANK], F32, name="bank%d" % b)

        best = {}

        def readings(s):
            cols = slice(s * P, (s + 1) * P)
            y2_sb = work.tile([P, S], F32, name="y2_sb")
            tone = keep.tile([P, S], F32, name="tone")
            top = feats.tile([P, S], F32, name="top")
            for h in range(S // BANK):
                js = slice(h * BANK, (h + 1) * BANK)
                moving = dict(rhs=v_codes[:, js].bitcast(FP8X4), rhs_scale=v_scales[:, js], start=True, stop=True)
                y2 = bank(2 + h)
                nc.tensor.matmul_mx(out=y2[:], lhsT=w2_codes[:, 2 * s * P : 2 * (s + 1) * P].bitcast(FP4X4), lhsT_scale=w2_sc[:, cols], **moving)
                y1 = bank(6 * (s % 2) + h)
                nc.tensor.matmul_mx(out=y1[:], lhsT=w_codes[1][:, cols].bitcast(FP8X4), lhsT_scale=w_scales[1][:, cols], **moving)
                y3 = bank(4 + h)
                nc.tensor.matmul_mx(out=y3[:], lhsT=w_codes[3][:, cols].bitcast(FP8X4), lhsT_scale=w_scales[3][:, cols], **moving)
                nc.scalar.copy(y2_sb[:, js], y2[:])
                nc.scalar.activation(tone[:, js], y3[:], ACT.Tanh)
                nc.vector.tensor_tensor(top[:, js], y1[:], y2_sb[:, js], ALU.max)
            nc.gpsimd.tensor_tensor(tone[:], tone[:], factors[s % PACK], ALU.mult)
            nc.gpsimd.tensor_tensor(top[:], top[:], tone[:], ALU.mult)
            best[s] = top

        def put(s):
            nc.vector.tensor_copy(page[s][:].indirect(idx3[:]), best[s][:])

        opened = {(a, h): kept([P, PACK, HALF], F32, "opened%d%d" % (a, h)) for a in range(2) for h in range(2)}
        x_codes = {(a, h): kept([P, HALF], U32, "x_codes%d%d" % (a, h)) for a in range(2) for h in range(2)}
        x_scales = {(a, h): kept([P, HALF], U8, "x_scales%d%d" % (a, h)) for a in range(2) for h in range(2)}

        def fetch(s):
            a, t = divmod(s, PACK)
            for h in range(2):
                listed = idx4[:, h * (HALF // 16) : (h + 1) * (HALF // 16)]
                nc.vector.tensor_copy(opened[a, h][:, t, :], page[s][:].indirect(listed))

        def quantise_x(a, h):
            grouped = work.tile([P, HALF * PACK], BF16, name="grouped", align_bytes=64)
            nc.scalar.activation(
                grouped[:].rearrange("p (c i t) -> p c t i", i=4, t=PACK),
                opened[a, h][:].rearrange("p t (c i) -> p c t i", i=4),
                ACT.Abs,
            )
            nc.vector.quantize_mx(out=x_codes[a, h][:].bitcast(FP8X4), scales=x_scales[a, h][:], in_=grouped[:])

        v2_scales = kept([P, S2], U8, "v2_scales")
        v2_codes = [kept([P, S2], U32, "v2_codes%d" % a) for a in range(2)]
        for n in (3, 1):
            quantise_weight(nc.vector.tensor_copy, n, 0, 0, 1)
        readings(0)
        nc.vector.tensor_copy(v2_scales[:], v2_plane[:].indirect(idx2[:]))
        for n in (3, 1):
            quantise_weight(nc.scalar.copy, n, 0, 1, PACK)
        readings(1)
        nc.vector.tensor_copy(v2_codes[0][:], v2_table[0][:].bitcast(U32).indirect(idx2[:]))

        for s in range(SLICES):
            put(s)
            fetch(s)
            if s == 0:
                nc.vector.tensor_copy(v2_codes[1][:], v2_table[1][:].bitcast(U32).indirect(idx2[:]))
                for n in (3, 1):
                    quantise_weight(nc.scalar.copy, n, 1, 0, PACK)
            if s == PACK:
                for g in range(2):
                    nc.scalar.mul(allowed[g][:], allowed[g][:], 0.5)
            if s == PACK - 1:
                for h in range(2):
                    quantise_x(0, h)
            if s + 2 < SLICES:
                readings(s + 2)

        def score_pass(e, h, pair, a):
            for i in range(2):
                ms = slice((2 * pair + i) * P, (2 * pair + i + 1) * P)
                nc.tensor.matmul_mx(
                    out=e[:, i * HALF : (i + 1) * HALF],
                    lhsT=v2_codes[a][:, ms].bitcast(FP8X4),
                    lhsT_scale=v2_scales[4 * a : P, ms],
                    rhs=x_codes[a, h][:].bitcast(FP8X4),
                    rhs_scale=x_scales[a, h][:],
                    start=(a == 0 and i == 0),
                    stop=(a == 1 and i == 1),
                )

        sums = {}
        for h in range(2):
            for pair in range(4):
                sums[h, pair] = bank(4 * h + pair)
                score_pass(sums[h, pair], h, pair, 0)
        for h in range(2):
            quantise_x(1, h)
        out_rows = out.rearrange("(c p) j -> p c j", p=P)
        for h in range(2):
            js = slice(h * HALF, (h + 1) * HALF)
            for pair in range(4):
                score_pass(sums[h, pair], h, pair, 1)
                score = pages.tile([P, 2, HALF], F32, name="page")
                g, c = divmod(2 * pair, PACK)
                last = h == 1 and pair == 3
                for i0, i1 in ((0, 1), (1, 2)) if last else ((0, 2),):
                    part = score[:, i0:i1, :]
                    nc.scalar.activation(part.rearrange("p i j -> p (i j)"), sums[h, pair][:, i0 * HALF : i1 * HALF], ACT.Tanh, scale=0.5)
                    nc.vector.scalar_tensor_tensor(part, part, 1.0, allowed[g][:, c + i0 : c + i1, js], ALU.add, ALU.mult)
                    nc.sync.dma_start(out_rows[:, 2 * pair + i0 : 2 * pair + i1, js], part)
